import numpy as np
import ml_dtypes


def mxq(x, axis, fmt="e4m3"):
    dtype, down = {"e4m3": (ml_dtypes.float8_e4m3fn, 7), "e5m2": (ml_dtypes.float8_e5m2, 14)}[fmt]
    v = np.moveaxis(np.asarray(x, np.float32).astype(ml_dtypes.bfloat16).astype(np.float64), axis, -1)
    blocks = v.reshape(v.shape[:-1] + (-1, 32))
    amax = np.abs(blocks).max(-1, keepdims=True)
    byte = np.maximum(np.where(amax > 0, np.frexp(amax)[1] - 1 + 127, 0) - down, 1)
    scale = np.exp2(byte - 127.0)
    codes = (blocks / scale).astype(np.float32).astype(dtype).astype(np.float64)
    return np.moveaxis((codes * scale).reshape(v.shape), -1, axis)


WIDE = False


def mx_kscale(k):
    if not WIDE:
        return np.ones(k)
    levels = np.array([10, -10, 5, -5, 0])
    if k % 512:
        return np.exp2(np.random.permutation(np.resize(levels, k // 32))).repeat(32)
    a = np.empty((k // 512, 16))
    for p in range(k // 512):
        a[p, :8] = np.random.permutation(np.resize(levels, 8))
        for g in range(8):
            far = levels[np.abs(levels - a[p, g]) >= 10]
            a[p, g + 8] = far[np.random.randint(len(far))]
    return np.exp2(a.ravel()).repeat(32)


def f64(x):
    return np.asarray(x).astype(np.float64)


def striped(idx):
    return np.tile(np.asarray(idx).reshape(-1, 16).T, (8, 1)).astype(np.uint16)


def unstriped(offs):
    return offs[:16].T.reshape(-1).astype(np.int64)


E2M1 = np.array([0.0, 0.5, 1.0, 1.5, 2.0, 3.0, 4.0, 6.0, -0.0, -0.5, -1.0, -1.5, -2.0, -3.0, -4.0, -6.0])


def pack_weight(w, fmt):
    k, n = w.shape
    w = f64(np.asarray(w, np.float32).astype(ml_dtypes.bfloat16)).reshape(k // 32, 32, n)
    amax = np.abs(w).max(1)
    if fmt == "e4m3":
        byte = np.frexp(amax)[1] - 1 + 127 - 7
    else:
        mant, ex = np.frexp(amax / 6.0)
        byte = np.where(mant > 0.5, ex, ex - 1) + 127
    byte = np.clip(np.where(amax > 0, byte, 1), 1, 254)
    scaled = (w * np.exp2(127.0 - byte)[:, None, :]).reshape(k, n).astype(np.float32)
    by_word = np.ascontiguousarray(scaled.reshape(k // 512, 128, 4, n).transpose(0, 1, 3, 2))
    if fmt == "e4m3":
        words = by_word.astype(ml_dtypes.float8_e4m3fn).view(np.uint8)
    else:
        c = by_word.astype(ml_dtypes.float4_e2m1fn).view(np.uint8) & 0xF
        words = (c[..., 0::2] | (c[..., 1::2] << 4)).reshape(k // 512, 128, 2 * n)
    return np.ascontiguousarray(words), np.ascontiguousarray(byte.astype(np.uint8).reshape(k // 512, 16, n))


def unpack_weight(words, scales, fmt):
    g, _, n = scales.shape
    words = np.ascontiguousarray(words).reshape(g, 128, n, -1)
    if fmt == "e4m3":
        vals = words.view(ml_dtypes.float8_e4m3fn).astype(np.float64)
    else:
        nib = np.empty((g, 128, n, 4), np.uint8)
        nib[..., 0::2] = words & 0xF
        nib[..., 1::2] = words >> 4
        vals = E2M1[nib]
    vals = vals * np.repeat(np.exp2(scales.astype(np.float64) - 127.0), 8, axis=1)[..., None]
    return vals.transpose(0, 1, 3, 2).reshape(g * 512, n)


D, E, T, I, G, U, Q = 512, 512, 2048, 512, 64, 512, 128


def setup_inputs():
    n = np.random.standard_normal
    idx = np.random.permutation(T)[:I]
    idx2 = np.random.permutation(U)[:G]
    fd = mx_kscale(D)
    fe = mx_kscale(E)
    pgsump = pack_weight(n((D, U)) / fd[:, None], "e2m1")
    keysp = pack_weight(n((D, T)) / fd[:, None], "e2m1")
    valsp = pack_weight(n((E, T)) / fe[:, None], "e2m1")
    return {
        "pquery": (n((D, Q)) * 1.0 / np.sqrt(D) * fd[:, None]).astype(np.float32),
        "pgsum_words": pgsump[0],
        "pgsum_scales": pgsump[1],
        "query": (n((D, Q)) * 0.7 / np.sqrt(D) * fd[:, None]).astype(np.float32),
        "keys_words": keysp[0],
        "keys_scales": keysp[1],
        "even": (np.random.uniform(0.1, 0.6, (Q, 1))).astype(np.float32),
        "gout": (n((E, Q)) * 1 / np.sqrt(E) * fe[:, None]).astype(np.float32),
        "vals_words": valsp[0],
        "vals_scales": valsp[1],
        "old": (0.5 * n((Q, T))).astype(np.float32),
        "offs": striped(idx),
        "offs2": striped(idx2),
    }


def reference(pquery, pgsum_words, pgsum_scales, query, keys_words, keys_scales, even, gout, vals_words, vals_scales, old, offs, offs2):
    idx = unstriped(offs)
    idx2 = unstriped(offs2)
    pgsumu = unpack_weight(pgsum_words, pgsum_scales, "e2m1")
    keysu = unpack_weight(keys_words, keys_scales, "e2m1")
    valsu = unpack_weight(vals_words, vals_scales, "e2m1")
    pqueryq = mxq(f64(pquery), 0, "e4m3")
    pgsumidx2g = pgsumu[:, idx2]
    b = pqueryq.T @ pgsumidx2g
    pb = np.exp(b - np.max(b, axis=1, keepdims=True))
    zb = np.sum(pb, axis=1, keepdims=True)
    queryq = mxq(f64(query), 0, "e4m3")
    keysidxg = keysu[:, idx]
    a = queryq.T @ keysidxg
    pa = np.exp(a)
    s = pa.reshape(Q, G, I // G).sum(axis=2)
    goutq = mxq(f64(gout), 0, "e4m3")
    valsidxg = valsu[:, idx]
    c0 = goutq.T @ valsidxg
    w = pb / zb * (1.0 - f64(even)) + f64(even) / 64.0
    e1 = w / s
    r1 = np.repeat(e1, I // G, axis=1)
    ds = w * (pa * c0).reshape(Q, G, I // G).sum(axis=2) / np.square(s) * (-1.0)
    r2 = np.repeat(ds, I // G, axis=1)
    dpa = r1 * c0 + r2
    da = dpa * pa
    gs = da * 1024.0
    gf = np.zeros((Q, T))
    gf[:, idx] = gs
    y = f64(old) + gf
    return y

@@ -1,0 +1,163 @@
+from contextlib import ExitStack
+
+import concourse.mybir as mybir
+
+D, T, SLOTS, PAGES, POOL_PAGES, Q = 512, 2048, 512, 64, 512, 128
+PER_PAGE = SLOTS // PAGES
+P = 128
+PACK = 4
+GAIN = 1024.0
+FLOPS = 2 * Q * D * (2 * SLOTS + PAGES)
+
+F32 = mybir.dt.float32
+BF16 = mybir.dt.bfloat16
+I32 = mybir.dt.int32
+U32 = mybir.dt.uint32
+U16 = mybir.dt.uint16
+U8 = mybir.dt.uint8
+FP8X4 = mybir.dt.float8_e4m3fn_x4
+FP4X4 = mybir.dt.float4_e2m1fn_x4
+ALU = mybir.AluOpType
+ACT = mybir.ActivationFunctionType
+AXIS_X = mybir.AxisListType.X
+
+STORE_WIDTHS = (256, 512, 512, 512, 256)
+
+
+def tile_attend_bevenmass_a_kernel(tc, pquery, pgsum_words, pgsum_scales, query, keys_words, keys_scales, even, gout,
+                                    vals_words, vals_scales, old, offs, offs2, out):
+    nc = tc.nc
+    with ExitStack() as ctx:
+        sb = ctx.enter_context(tc.tile_pool(name="sb", bufs=1))
+        ps = ctx.enter_context(tc.psum_pool(name="ps", bufs=1))
+
+        def zeroed_plane(name, width):
+            plane = sb.tile([P, width], U8, name=name, align_bytes=64)
+            nc.vector.memset(plane[:].bitcast(I32), 0)
+            return plane
+
+        def load_words(name, words, width):
+            tile = sb.tile([P, width], U16, name=name, align_bytes=64)
+            nc.sync.dma_start(out=tile[:].bitcast(I32), in_=words[0].bitcast(I32))
+            return tile
+
+        def load_scales(plane, scales):
+            for r in range(4):
+                nc.sync.dma_start(out=plane[r:P:32, :].bitcast(I32), in_=scales[0, r:16:4, :].bitcast(I32))
+
+        def load_rows(name, x):
+            raw = sb.tile([P, PACK, Q], F32, name=name)
+            nc.sync.dma_start(out=raw[:], in_=x.rearrange("(p j) q -> p j q", j=PACK))
+            return raw
+
+        def interleave(name, raw):
+            grouped = sb.tile([P, Q, PACK], BF16, name=name, align_bytes=64)
+            nc.scalar.activation(
+                out=grouped[:].rearrange("p (c i) t -> p c t i", i=4),
+                in_=raw[:].rearrange("p t (c i) -> p c t i", i=4),
+                func=ACT.Copy,
+            )
+            return grouped
+
+        def quantize(name, grouped):
+            codes = sb.tile([P, Q], U32, name=name + "_codes", align_bytes=64)
+            scales = sb.tile([P, Q], U8, name=name + "_scales", align_bytes=64)
+            nc.vector.quantize_mx(out=codes[:].bitcast(FP8X4), scales=scales[:], in_=grouped[:].rearrange("p q t -> p (q t)"))
+            return codes, scales
+
+        def gather(name, window, offsets, n, dtype):
+            picked = sb.tile([P, n], dtype, name=name, align_bytes=64)
+            nc.vector.tensor_copy(picked[:], window[:].indirect(offsets[:]))
+            return picked
+
+        def product(name, rows, words, scales, n):
+            acc = ps.tile([P, n], F32, name=name)
+            nc.tensor.matmul_mx(out=acc[:], lhsT=rows[0][:].bitcast(FP8X4), lhsT_scale=rows[1][:],
+                                rhs=words[:].bitcast(FP4X4), rhs_scale=scales[:], start=True, stop=True)
+            return acc
+
+        def by_page(ap):
+            return ap.rearrange("p (g j) -> p g j", j=PER_PAGE)
+
+        def spread(ap):
+            return ap.unsqueeze(2).to_broadcast([P, PAGES, PER_PAGE])
+
+        key_plane = zeroed_plane("key_plane", T)
+        val_plane = zeroed_plane("val_plane", T)
+        page_plane = zeroed_plane("page_plane", POOL_PAGES)
+        gf = sb.tile([P, T], F32, name="gf")
+        nc.vector.memset(gf[:], 0.0)
+
+        slots = sb.tile([P, SLOTS // 16], U16, name="slots")
+        nc.sync.dma_start(slots[:], offs)
+        key_pool = load_words("key_pool", keys_words, T)
+        load_scales(key_plane, keys_scales)
+        query_raw = load_rows("query_raw", query)
+        val_pool = load_words("val_pool", vals_words, T)
+        load_scales(val_plane, vals_scales)
+        gout_raw = load_rows("gout_raw", gout)
+        pages = sb.tile([P, PAGES // 16], U16, name="pages")
+        nc.sync.dma_start(pages[:], offs2)
+        page_pool = load_words("page_pool", pgsum_words, POOL_PAGES)
+        pquery_raw = load_rows("pquery_raw", pquery)
+        load_scales(page_plane, pgsum_scales)
+        ev = sb.tile([P, 1], F32, name="ev")
+        nc.sync.dma_start(out=ev[:], in_=even)
+        res = sb.tile([P, T], F32, name="res")
+        nc.sync.dma_start(out=res[:], in_=old)
+
+        key_words = gather("key_words", key_pool, slots, SLOTS, U16)
+        key_scales = gather("key_scales", key_plane, slots, SLOTS, U8)
+        a = product("a", quantize("query", interleave("query_bf", query_raw)), key_words, key_scales, SLOTS)
+        pa = sb.tile([P, SLOTS], F32, name="pa")
+        nc.scalar.activation(out=pa[:], in_=a[:], func=ACT.Exp)
+
+        val_words = gather("val_words", val_pool, slots, SLOTS, U16)
+        val_scales = gather("val_scales", val_plane, slots, SLOTS, U8)
+        c0 = product("c0", quantize("gout", interleave("gout_bf", gout_raw)), val_words, val_scales, SLOTS)
+
+        page_words = gather("page_words", page_pool, pages, PAGES, U16)
+        page_scales = gather("page_scales", page_plane, pages, PAGES, U8)
+        b = product("b", quantize("pquery", interleave("pquery_bf", pquery_raw)), page_words, page_scales, PAGES)
+
+        s = sb.tile([P, PAGES], F32, name="s")
+        nc.vector.tensor_reduce(out=s[:], in_=by_page(pa[:]), axis=AXIS_X, op=ALU.add)
+        pc = sb.tile([P, SLOTS], F32, name="pc")
+        nc.vector.tensor_tensor(out=pc[:], in0=c0[:], in1=pa[:], op=ALU.mult)
+        neg_max = sb.tile([P, 1], F32, name="neg_max")
+        nc.vector.tensor_reduce(out=neg_max[:], in_=b[:], axis=AXIS_X, op=ALU.max, negate=True)
+        pb = sb.tile([P, PAGES], F32, name="pb")
+        zb = sb.tile([P, 1], F32, name="zb")
+        nc.scalar.activation(out=pb[:], in_=b[:], func=ACT.Exp, bias=neg_max[:], accum_out=zb[:])
+        inv_s = sb.tile([P, PAGES], F32, name="inv_s")
+        nc.vector.reciprocal(out=inv_s[:], in_=s[:])
+        u = sb.tile([P, PAGES], F32, name="u")
+        nc.vector.tensor_reduce(out=u[:], in_=by_page(pc[:]), axis=AXIS_X, op=ALU.add)
+        inv_z = sb.tile([P, 1], F32, name="inv_z")
+        nc.vector.reciprocal(out=inv_z[:], in_=zb[:])
+
+        rest = sb.tile([P, 1], F32, name="rest")
+        nc.scalar.activation(out=rest[:], in_=ev[:], func=ACT.Copy, scale=-GAIN, bias=GAIN)
+        floor = sb.tile([P, 1], F32, name="floor")
+        nc.scalar.activation(out=floor[:], in_=ev[:], func=ACT.Copy, scale=GAIN / PAGES)
+        coef = sb.tile([P, 1], F32, name="coef")
+        nc.scalar.activation(out=coef[:], in_=rest[:], func=ACT.Copy, scale=inv_z[:])
+        w = sb.tile([P, PAGES], F32, name="w")
+        nc.scalar.activation(out=w[:], in_=pb[:], func=ACT.Identity, scale=coef[:], bias=floor[:])
+
+        mean = sb.tile([P, PAGES], F32, name="mean")
+        nc.vector.tensor_tensor(out=mean[:], in0=u[:], in1=inv_s[:], op=ALU.mult)
+        e1 = sb.tile([P, PAGES], F32, name="e1")
+        nc.vector.tensor_tensor(out=e1[:], in0=w[:], in1=inv_s[:], op=ALU.mult)
+        centred = sb.tile([P, SLOTS], F32, name="centred")
+        nc.vector.tensor_tensor(out=by_page(centred[:]), in0=by_page(c0[:]), in1=spread(mean[:]), op=ALU.subtract)
+        share = sb.tile([P, SLOTS], F32, name="share")
+        nc.vector.tensor_tensor(out=by_page(share[:]), in0=by_page(pa[:]), in1=spread(e1[:]), op=ALU.mult)
+        nc.vector.tensor_tensor(gf[:].indirect(slots[:]), centred[:], share[:], ALU.mult)
+
+        start = 0
+        for width in STORE_WIDTHS:
+            cols = slice(start, start + width)
+            nc.vector.tensor_tensor(out=res[:, cols], in0=res[:, cols], in1=gf[:, cols], op=ALU.add)
+            nc.sync.dma_start(out=out[:, cols], in_=res[:, cols])
+            start += width

@@ -41,17 +41,17 @@ def tile_attend_bevenmass_a_kernel(tc, pquery, pgsum_words, pgsum_scales, query,
             nc.sync.dma_start(out=tile[:].bitcast(I32), in_=words[0].bitcast(I32))
             return tile
 
-        def load_scales(plane, scales):
+        def load_scales(queue, plane, scales):
             for r in range(4):
-                nc.sync.dma_start(out=plane[r:P:32, :].bitcast(I32), in_=scales[0, r:16:4, :].bitcast(I32))
+                queue.dma_start(out=plane[r:P:32, :].bitcast(I32), in_=scales[0, r:16:4, :].bitcast(I32))
 
         def load_rows(name, x):
-            raw = sb.tile([P, PACK, Q], F32, name=name)
+            raw = sb.tile([P, PACK, Q], F32, name=name, tag=name)
             nc.sync.dma_start(out=raw[:], in_=x.rearrange("(p j) q -> p j q", j=PACK))
             return raw
 
         def interleave(name, raw):
-            grouped = sb.tile([P, Q, PACK], BF16, name=name, align_bytes=64)
+            grouped = sb.tile([P, Q, PACK], BF16, name=name, tag=name, align_bytes=64)
             nc.scalar.activation(
                 out=grouped[:].rearrange("p (c i) t -> p c t i", i=4),
                 in_=raw[:].rearrange("p t (c i) -> p c t i", i=4),
@@ -91,16 +91,16 @@ def tile_attend_bevenmass_a_kernel(tc, pquery, pgsum_words, pgsum_scales, query,
         slots = sb.tile([P, SLOTS // 16], U16, name="slots")
         nc.sync.dma_start(slots[:], offs)
         key_pool = load_words("key_pool", keys_words, T)
-        load_scales(key_plane, keys_scales)
+        load_scales(nc.sync, key_plane, keys_scales)
         query_raw = load_rows("query_raw", query)
         val_pool = load_words("val_pool", vals_words, T)
-        load_scales(val_plane, vals_scales)
+        load_scales(nc.sync, val_plane, vals_scales)
         gout_raw = load_rows("gout_raw", gout)
+        pquery_raw = load_rows("pquery_raw", pquery)
+        page_pool = load_words("page_pool", pgsum_words, POOL_PAGES)
         pages = sb.tile([P, PAGES // 16], U16, name="pages")
         nc.sync.dma_start(pages[:], offs2)
-        page_pool = load_words("page_pool", pgsum_words, POOL_PAGES)
-        pquery_raw = load_rows("pquery_raw", pquery)
-        load_scales(page_plane, pgsum_scales)
+        load_scales(nc.gpsimd, page_plane, pgsum_scales)
         ev = sb.tile([P, 1], F32, name="ev")
         nc.sync.dma_start(out=ev[:], in_=even)
         res = sb.tile([P, T], F32, name="res")
@@ -109,8 +109,6 @@ def tile_attend_bevenmass_a_kernel(tc, pquery, pgsum_words, pgsum_scales, query,
         key_words = gather("key_words", key_pool, slots, SLOTS, U16)
         key_scales = gather("key_scales", key_plane, slots, SLOTS, U8)
         a = product("a", quantize("query", interleave("query_bf", query_raw)), key_words, key_scales, SLOTS)
-        pa = sb.tile([P, SLOTS], F32, name="pa")
-        nc.scalar.activation(out=pa[:], in_=a[:], func=ACT.Exp)
 
         val_words = gather("val_words", val_pool, slots, SLOTS, U16)
         val_scales = gather("val_scales", val_plane, slots, SLOTS, U8)
@@ -119,36 +117,37 @@ def tile_attend_bevenmass_a_kernel(tc, pquery, pgsum_words, pgsum_scales, query,
         page_words = gather("page_words", page_pool, pages, PAGES, U16)
         page_scales = gather("page_scales", page_plane, pages, PAGES, U8)
         b = product("b", quantize("pquery", interleave("pquery_bf", pquery_raw)), page_words, page_scales, PAGES)
+        pa = sb.tile([P, SLOTS], F32, name="pa", tag="pquery_raw")
+        nc.scalar.activation(out=pa[:], in_=a[:], func=ACT.Exp)
 
         s = sb.tile([P, PAGES], F32, name="s")
         nc.vector.tensor_reduce(out=s[:], in_=by_page(pa[:]), axis=AXIS_X, op=ALU.add)
-        pc = sb.tile([P, SLOTS], F32, name="pc")
-        nc.vector.tensor_tensor(out=pc[:], in0=c0[:], in1=pa[:], op=ALU.mult)
         neg_max = sb.tile([P, 1], F32, name="neg_max")
         nc.vector.tensor_reduce(out=neg_max[:], in_=b[:], axis=AXIS_X, op=ALU.max, negate=True)
         pb = sb.tile([P, PAGES], F32, name="pb")
         zb = sb.tile([P, 1], F32, name="zb")
         nc.scalar.activation(out=pb[:], in_=b[:], func=ACT.Exp, bias=neg_max[:], accum_out=zb[:])
+        rest = sb.tile([P, 1], F32, name="rest")
+        nc.scalar.activation(out=rest[:], in_=ev[:], func=ACT.Copy, scale=-GAIN, bias=GAIN)
+        floor = sb.tile([P, 1], F32, name="floor")
+        nc.scalar.activation(out=floor[:], in_=ev[:], func=ACT.Copy, scale=GAIN / PAGES)
+        floor_z = sb.tile([P, 1], F32, name="floor_z")
+        nc.scalar.activation(out=floor_z[:], in_=zb[:], func=ACT.Copy, scale=floor[:])
+        wz = sb.tile([P, PAGES], F32, name="wz")
+        nc.scalar.activation(out=wz[:], in_=pb[:], func=ACT.Identity, scale=rest[:], bias=floor_z[:])
+
+        pc = sb.tile([P, SLOTS], F32, name="pc")
+        nc.vector.tensor_tensor(out=pc[:], in0=c0[:], in1=pa[:], op=ALU.mult)
         inv_s = sb.tile([P, PAGES], F32, name="inv_s")
         nc.vector.reciprocal(out=inv_s[:], in_=s[:])
         u = sb.tile([P, PAGES], F32, name="u")
         nc.vector.tensor_reduce(out=u[:], in_=by_page(pc[:]), axis=AXIS_X, op=ALU.add)
         inv_z = sb.tile([P, 1], F32, name="inv_z")
         nc.vector.reciprocal(out=inv_z[:], in_=zb[:])
-
-        rest = sb.tile([P, 1], F32, name="rest")
-        nc.scalar.activation(out=rest[:], in_=ev[:], func=ACT.Copy, scale=-GAIN, bias=GAIN)
-        floor = sb.tile([P, 1], F32, name="floor")
-        nc.scalar.activation(out=floor[:], in_=ev[:], func=ACT.Copy, scale=GAIN / PAGES)
-        coef = sb.tile([P, 1], F32, name="coef")
-        nc.scalar.activation(out=coef[:], in_=rest[:], func=ACT.Copy, scale=inv_z[:])
-        w = sb.tile([P, PAGES], F32, name="w")
-        nc.scalar.activation(out=w[:], in_=pb[:], func=ACT.Identity, scale=coef[:], bias=floor[:])
-
         mean = sb.tile([P, PAGES], F32, name="mean")
         nc.vector.tensor_tensor(out=mean[:], in0=u[:], in1=inv_s[:], op=ALU.mult)
         e1 = sb.tile([P, PAGES], F32, name="e1")
-        nc.vector.tensor_tensor(out=e1[:], in0=w[:], in1=inv_s[:], op=ALU.mult)
+        nc.vector.scalar_tensor_tensor(out=e1[:], in0=wz[:], scalar=inv_z[:], in1=inv_s[:], op0=ALU.mult, op1=ALU.mult)
         centred = sb.tile([P, SLOTS], F32, name="centred")
         nc.vector.tensor_tensor(out=by_page(centred[:]), in0=by_page(c0[:]), in1=spread(mean[:]), op=ALU.subtract)
         share = sb.tile([P, SLOTS], F32, name="share")

from contextlib import ExitStack

import concourse.mybir as mybir

D, T, SLOTS, PAGES, POOL_PAGES, Q = 512, 2048, 512, 64, 512, 128
PER_PAGE = SLOTS // PAGES
P = 128
PACK = 4
GAIN = 1024.0
FLOPS = 2 * Q * D * (2 * SLOTS + PAGES)

F32 = mybir.dt.float32
BF16 = mybir.dt.bfloat16
I32 = mybir.dt.int32
U32 = mybir.dt.uint32
U16 = mybir.dt.uint16
U8 = mybir.dt.uint8
FP8X4 = mybir.dt.float8_e4m3fn_x4
FP4X4 = mybir.dt.float4_e2m1fn_x4
ALU = mybir.AluOpType
ACT = mybir.ActivationFunctionType
AXIS_X = mybir.AxisListType.X

STORE_WIDTHS = (256, 512, 512, 512, 256)


def tile_attend_bevenmass_a_kernel(tc, pquery, pgsum_words, pgsum_scales, query, keys_words, keys_scales, even, gout,
                                    vals_words, vals_scales, old, offs, offs2, out):
    nc = tc.nc
    with ExitStack() as ctx:
        sb = ctx.enter_context(tc.tile_pool(name="sb", bufs=1))
        ps = ctx.enter_context(tc.psum_pool(name="ps", bufs=1))

        def zeroed_plane(name, width):
            plane = sb.tile([P, width], U8, name=name, align_bytes=64)
            nc.vector.memset(plane[:].bitcast(I32), 0)
            return plane

        def load_words(name, words, width):
            tile = sb.tile([P, width], U16, name=name, align_bytes=64)
            nc.sync.dma_start(out=tile[:].bitcast(I32), in_=words[0].bitcast(I32))
            return tile

        def load_scales(queue, plane, scales):
            for r in range(4):
                queue.dma_start(out=plane[r:P:32, :].bitcast(I32), in_=scales[0, r:16:4, :].bitcast(I32))

        def load_rows(name, x):
            raw = sb.tile([P, PACK, Q], F32, name=name, tag=name)
            nc.sync.dma_start(out=raw[:], in_=x.rearrange("(p j) q -> p j q", j=PACK))
            return raw

        def interleave(name, raw):
            grouped = sb.tile([P, Q, PACK], BF16, name=name, tag=name, align_bytes=64)
            nc.scalar.activation(
                out=grouped[:].rearrange("p (c i) t -> p c t i", i=4),
                in_=raw[:].rearrange("p t (c i) -> p c t i", i=4),
                func=ACT.Copy,
            )
            return grouped

        def quantize(name, grouped):
            codes = sb.tile([P, Q], U32, name=name + "_codes", align_bytes=64)
            scales = sb.tile([P, Q], U8, name=name + "_scales", align_bytes=64)
            nc.vector.quantize_mx(out=codes[:].bitcast(FP8X4), scales=scales[:], in_=grouped[:].rearrange("p q t -> p (q t)"))
            return codes, scales

        def gather(name, window, offsets, n, dtype):
            picked = sb.tile([P, n], dtype, name=name, align_bytes=64)
            nc.vector.tensor_copy(picked[:], window[:].indirect(offsets[:]))
            return picked

        def product(name, rows, words, scales, n):
            acc = ps.tile([P, n], F32, name=name)
            nc.tensor.matmul_mx(out=acc[:], lhsT=rows[0][:].bitcast(FP8X4), lhsT_scale=rows[1][:],
                                rhs=words[:].bitcast(FP4X4), rhs_scale=scales[:], start=True, stop=True)
            return acc

        def by_page(ap):
            return ap.rearrange("p (g j) -> p g j", j=PER_PAGE)

        def spread(ap):
            return ap.unsqueeze(2).to_broadcast([P, PAGES, PER_PAGE])

        key_plane = zeroed_plane("key_plane", T)
        val_plane = zeroed_plane("val_plane", T)
        page_plane = zeroed_plane("page_plane", POOL_PAGES)
        gf = sb.tile([P, T], F32, name="gf")
        nc.vector.memset(gf[:], 0.0)

        slots = sb.tile([P, SLOTS // 16], U16, name="slots")
        nc.sync.dma_start(slots[:], offs)
        key_pool = load_words("key_pool", keys_words, T)
        load_scales(nc.sync, key_plane, keys_scales)
        query_raw = load_rows("query_raw", query)
        val_pool = load_words("val_pool", vals_words, T)
        load_scales(nc.sync, val_plane, vals_scales)
        gout_raw = load_rows("gout_raw", gout)
        pquery_raw = load_rows("pquery_raw", pquery)
        page_pool = load_words("page_pool", pgsum_words, POOL_PAGES)
        pages = sb.tile([P, PAGES // 16], U16, name="pages")
        nc.sync.dma_start(pages[:], offs2)
        load_scales(nc.gpsimd, page_plane, pgsum_scales)
        ev = sb.tile([P, 1], F32, name="ev")
        nc.sync.dma_start(out=ev[:], in_=even)
        res = sb.tile([P, T], F32, name="res")
        nc.sync.dma_start(out=res[:], in_=old)

        key_words = gather("key_words", key_pool, slots, SLOTS, U16)
        key_scales = gather("key_scales", key_plane, slots, SLOTS, U8)
        a = product("a", quantize("query", interleave("query_bf", query_raw)), key_words, key_scales, SLOTS)

        val_words = gather("val_words", val_pool, slots, SLOTS, U16)
        val_scales = gather("val_scales", val_plane, slots, SLOTS, U8)
        c0 = product("c0", quantize("gout", interleave("gout_bf", gout_raw)), val_words, val_scales, SLOTS)

        page_words = gather("page_words", page_pool, pages, PAGES, U16)
        page_scales = gather("page_scales", page_plane, pages, PAGES, U8)
        b = product("b", quantize("pquery", interleave("pquery_bf", pquery_raw)), page_words, page_scales, PAGES)
        pa = sb.tile([P, SLOTS], F32, name="pa", tag="pquery_raw")
        nc.scalar.activation(out=pa[:], in_=a[:], func=ACT.Exp)

        s = sb.tile([P, PAGES], F32, name="s")
        nc.vector.tensor_reduce(out=s[:], in_=by_page(pa[:]), axis=AXIS_X, op=ALU.add)
        neg_max = sb.tile([P, 1], F32, name="neg_max")
        nc.vector.tensor_reduce(out=neg_max[:], in_=b[:], axis=AXIS_X, op=ALU.max, negate=True)
        pb = sb.tile([P, PAGES], F32, name="pb")
        zb = sb.tile([P, 1], F32, name="zb")
        nc.scalar.activation(out=pb[:], in_=b[:], func=ACT.Exp, bias=neg_max[:], accum_out=zb[:])
        rest = sb.tile([P, 1], F32, name="rest")
        nc.scalar.activation(out=rest[:], in_=ev[:], func=ACT.Copy, scale=-GAIN, bias=GAIN)
        floor = sb.tile([P, 1], F32, name="floor")
        nc.scalar.activation(out=floor[:], in_=ev[:], func=ACT.Copy, scale=GAIN / PAGES)
        floor_z = sb.tile([P, 1], F32, name="floor_z")
        nc.scalar.activation(out=floor_z[:], in_=zb[:], func=ACT.Copy, scale=floor[:])
        wz = sb.tile([P, PAGES], F32, name="wz")
        nc.scalar.activation(out=wz[:], in_=pb[:], func=ACT.Identity, scale=rest[:], bias=floor_z[:])

        pc = sb.tile([P, SLOTS], F32, name="pc")
        nc.vector.tensor_tensor(out=pc[:], in0=c0[:], in1=pa[:], op=ALU.mult)
        inv_s = sb.tile([P, PAGES], F32, name="inv_s")
        nc.vector.reciprocal(out=inv_s[:], in_=s[:])
        u = sb.tile([P, PAGES], F32, name="u")
        nc.vector.tensor_reduce(out=u[:], in_=by_page(pc[:]), axis=AXIS_X, op=ALU.add)
        inv_z = sb.tile([P, 1], F32, name="inv_z")
        nc.vector.reciprocal(out=inv_z[:], in_=zb[:])
        mean = sb.tile([P, PAGES], F32, name="mean")
        nc.vector.tensor_tensor(out=mean[:], in0=u[:], in1=inv_s[:], op=ALU.mult)
        e1 = sb.tile([P, PAGES], F32, name="e1")
        nc.vector.scalar_tensor_tensor(out=e1[:], in0=wz[:], scalar=inv_z[:], in1=inv_s[:], op0=ALU.mult, op1=ALU.mult)
        centred = sb.tile([P, SLOTS], F32, name="centred")
        nc.vector.tensor_tensor(out=by_page(centred[:]), in0=by_page(c0[:]), in1=spread(mean[:]), op=ALU.subtract)
        share = sb.tile([P, SLOTS], F32, name="share")
        nc.vector.tensor_tensor(out=by_page(share[:]), in0=by_page(pa[:]), in1=spread(e1[:]), op=ALU.mult)
        nc.vector.tensor_tensor(gf[:].indirect(slots[:]), centred[:], share[:], ALU.mult)

        start = 0
        for width in STORE_WIDTHS:
            cols = slice(start, start + width)
            nc.vector.tensor_tensor(out=res[:, cols], in0=res[:, cols], in1=gf[:, cols], op=ALU.add)
            nc.sync.dma_start(out=out[:, cols], in_=res[:, cols])
            start += width
